import numpy as np, ml_dtypes
CORES = [0,1,2,3,8,9,10,11,16,17,18,19,24,25,26,27]
N = 16
def setup_inputs(rng):
    return {"x": rng.standard_normal((N, 128, 256), dtype=np.float32).astype(ml_dtypes.bfloat16)}
def reference(x):
    b = 256 // N
    blocks = x.reshape(N, 128, N, b)
    return {"y": np.ascontiguousarray(blocks.transpose(2, 1, 0, 3)).reshape(N, 128, 256)}

@@ -1,0 +1,69 @@
+from concourse.bass import DstId, RemoteDMATransfer
+
+SCRATCH = {
+    "xs": ("sbuf", [128, 256], "bfloat16"),
+    "land": ("sbuf", [128, 256], "bfloat16"),
+    "gw": ("sbuf", [128, 64], "bfloat16"),
+    "sp": ("sbuf", [128, 64], "bfloat16"),
+}
+SEMAPHORES = ["loaded", "own", "stored", "fed", "arrived", "sent"]
+
+
+def blk(r):
+    return slice(16 * r, 16 * r + 16)
+
+
+def cols(chip):
+    return slice(64 * chip, 64 * chip + 64)
+
+
+def rank_program(g, core, T, topo):
+    chip, k = divmod(core, 8)
+    P, M, D = chip ^ 2, chip ^ 1, chip ^ 3
+    sem = T.sem
+
+    def xfer(src, dst_core, dst, mask, remote_sem):
+        rid, pid, ring = topo.addr(dst_core)
+        return RemoteDMATransfer(dst_ids=[DstId(rid=rid, pnc=pid)], dma_engine_mask=mask,
+                                 remote_sem=remote_sem, src=src, dst=dst)
+
+    def deal(buf, c0, dst_chip, src_rank, first_engine):
+        return [xfer(buf[:, c0 + 16 * q:c0 + 16 * q + 16], 8 * dst_chip + q, T.land[:, blk(src_rank)],
+                     3 << (first_engine + 2 * q), sem.arrived) for q in range(4)]
+
+    if k >= 4:
+        h = k & 1
+        if k < 6:
+            out = deal(T.gw, 0, P, 4 * chip + 2 + h, 0) + deal(T.sp, 0, chip, 4 * M + 2 + h, 8)
+        else:
+            out = deal(T.gw, 0, M, 4 * chip + h, 0) + deal(T.sp, 0, chip, 4 * D + 2 + h, 8)
+        g.wait_ge(sem.fed, 8 + 4)
+        g.remote_dma_fused(out, local_sem=sem.sent)
+        g.wait_ge(sem.sent, 16)
+        return
+
+    r = 4 * chip + k
+    g.dma_start(T.xs[:], T.x[:]).then_inc(sem.loaded, 16)
+    g.wait_ge(sem.loaded, 16)
+
+    on_chip = [xfer(T.xs[:, blk(4 * chip + (k + d) % 4)], 8 * chip + (k + d) % 4, T.land[:, blk(r)],
+                    (0x0300, 0x0C00, 0xF000)[d - 1], sem.arrived) for d in (1, 2, 3)]
+
+    if k < 2:
+        g.remote_dma_fused([xfer(T.xs[:, cols(M)], 8 * chip + 6 + k, T.gw[:], 0x00FF, sem.fed),
+                            xfer(T.xs[:, cols(D)], 8 * chip + 2 + k, T.gw[:], 0xFF00, sem.fed)], local_sem=sem.sent)
+        g.remote_dma_fused(deal(T.xs, 64 * P, P, r, 0) + on_chip, local_sem=sem.sent)
+        g.dma_start(T.land[:, blk(r)], T.x[:, blk(r)]).then_inc(sem.own, 16)
+    else:
+        g.remote_dma_fused([xfer(T.xs[:, cols(M)], 8 * M + 2 + k, T.sp[:], 0x000F, sem.fed),
+                            xfer(T.xs[:, cols(D)], 8 * D + 4 + k, T.sp[:], 0x00F0, sem.fed),
+                            xfer(T.xs[:, cols(P)], 8 * chip + 2 + k, T.gw[:], 0xFF00, sem.fed)], local_sem=sem.sent)
+        g.dma_start(T.land[:, blk(r)], T.x[:, blk(r)]).then_inc(sem.own, 16)
+        g.wait_ge(sem.fed, 8)
+        g.remote_dma_fused(deal(T.gw, 0, D, r - 2, 0) + on_chip, local_sem=sem.sent)
+
+    g.wait_ge(sem.arrived, 32)
+    g.wait_ge(sem.own, 16)
+    g.dma_start(T.y[:], T.land[:]).then_inc(sem.stored, 16)
+    g.wait_ge(sem.stored, 16)
+    g.wait_ge(sem.sent, 32)

@@ -6,7 +6,7 @@ SCRATCH = {
     "gw": ("sbuf", [128, 64], "bfloat16"),
     "sp": ("sbuf", [128, 64], "bfloat16"),
 }
-SEMAPHORES = ["loaded", "own", "stored", "fed", "arrived", "sent"]
+SEMAPHORES = ["loaded", "own", "stored", "fed", "come", "arrived", "sent"]
 
 
 def blk(r):
@@ -33,12 +33,13 @@ def rank_program(g, core, T, topo):
 
     if k >= 4:
         h = k & 1
+        g.wait_ge(sem.fed, 8)
         if k < 6:
-            out = deal(T.gw, 0, P, 4 * chip + 2 + h, 0) + deal(T.sp, 0, chip, 4 * M + 2 + h, 8)
+            g.remote_dma_fused(deal(T.gw, 0, P, 4 * chip + 2 + h, 0), local_sem=sem.sent)
         else:
-            out = deal(T.gw, 0, M, 4 * chip + h, 0) + deal(T.sp, 0, chip, 4 * D + 2 + h, 8)
-        g.wait_ge(sem.fed, 8 + 4)
-        g.remote_dma_fused(out, local_sem=sem.sent)
+            g.remote_dma_fused(deal(T.gw, 0, M, 4 * chip + h, 0), local_sem=sem.sent)
+        g.wait_ge(sem.come, 4)
+        g.remote_dma_fused(deal(T.sp, 0, chip, 4 * (M if k < 6 else D) + 2 + h, 8), local_sem=sem.sent)
         g.wait_ge(sem.sent, 16)
         return
 
@@ -55,8 +56,8 @@ def rank_program(g, core, T, topo):
         g.remote_dma_fused(deal(T.xs, 64 * P, P, r, 0) + on_chip, local_sem=sem.sent)
         g.dma_start(T.land[:, blk(r)], T.x[:, blk(r)]).then_inc(sem.own, 16)
     else:
-        g.remote_dma_fused([xfer(T.xs[:, cols(M)], 8 * M + 2 + k, T.sp[:], 0x000F, sem.fed),
-                            xfer(T.xs[:, cols(D)], 8 * D + 4 + k, T.sp[:], 0x00F0, sem.fed),
+        g.remote_dma_fused([xfer(T.xs[:, cols(M)], 8 * M + 2 + k, T.sp[:], 0x000F, sem.come),
+                            xfer(T.xs[:, cols(D)], 8 * D + 4 + k, T.sp[:], 0x00F0, sem.come),
                             xfer(T.xs[:, cols(P)], 8 * chip + 2 + k, T.gw[:], 0xFF00, sem.fed)], local_sem=sem.sent)
         g.dma_start(T.land[:, blk(r)], T.x[:, blk(r)]).then_inc(sem.own, 16)
         g.wait_ge(sem.fed, 8)

from concourse.bass import DstId, RemoteDMATransfer

SCRATCH = {
    "xs": ("sbuf", [128, 256], "bfloat16"),
    "land": ("sbuf", [128, 256], "bfloat16"),
    "gw": ("sbuf", [128, 64], "bfloat16"),
    "sp": ("sbuf", [128, 64], "bfloat16"),
}
SEMAPHORES = ["loaded", "own", "stored", "fed", "come", "arrived", "sent"]


def blk(r):
    return slice(16 * r, 16 * r + 16)


def cols(chip):
    return slice(64 * chip, 64 * chip + 64)


def rank_program(g, core, T, topo):
    chip, k = divmod(core, 8)
    P, M, D = chip ^ 2, chip ^ 1, chip ^ 3
    sem = T.sem

    def xfer(src, dst_core, dst, mask, remote_sem):
        rid, pid, ring = topo.addr(dst_core)
        return RemoteDMATransfer(dst_ids=[DstId(rid=rid, pnc=pid)], dma_engine_mask=mask,
                                 remote_sem=remote_sem, src=src, dst=dst)

    def deal(buf, c0, dst_chip, src_rank, first_engine):
        return [xfer(buf[:, c0 + 16 * q:c0 + 16 * q + 16], 8 * dst_chip + q, T.land[:, blk(src_rank)],
                     3 << (first_engine + 2 * q), sem.arrived) for q in range(4)]

    if k >= 4:
        h = k & 1
        g.wait_ge(sem.fed, 8)
        if k < 6:
            g.remote_dma_fused(deal(T.gw, 0, P, 4 * chip + 2 + h, 0), local_sem=sem.sent)
        else:
            g.remote_dma_fused(deal(T.gw, 0, M, 4 * chip + h, 0), local_sem=sem.sent)
        g.wait_ge(sem.come, 4)
        g.remote_dma_fused(deal(T.sp, 0, chip, 4 * (M if k < 6 else D) + 2 + h, 8), local_sem=sem.sent)
        g.wait_ge(sem.sent, 16)
        return

    r = 4 * chip + k
    g.dma_start(T.xs[:], T.x[:]).then_inc(sem.loaded, 16)
    g.wait_ge(sem.loaded, 16)

    on_chip = [xfer(T.xs[:, blk(4 * chip + (k + d) % 4)], 8 * chip + (k + d) % 4, T.land[:, blk(r)],
                    (0x0300, 0x0C00, 0xF000)[d - 1], sem.arrived) for d in (1, 2, 3)]

    if k < 2:
        g.remote_dma_fused([xfer(T.xs[:, cols(M)], 8 * chip + 6 + k, T.gw[:], 0x00FF, sem.fed),
                            xfer(T.xs[:, cols(D)], 8 * chip + 2 + k, T.gw[:], 0xFF00, sem.fed)], local_sem=sem.sent)
        g.remote_dma_fused(deal(T.xs, 64 * P, P, r, 0) + on_chip, local_sem=sem.sent)
        g.dma_start(T.land[:, blk(r)], T.x[:, blk(r)]).then_inc(sem.own, 16)
    else:
        g.remote_dma_fused([xfer(T.xs[:, cols(M)], 8 * M + 2 + k, T.sp[:], 0x000F, sem.come),
                            xfer(T.xs[:, cols(D)], 8 * D + 4 + k, T.sp[:], 0x00F0, sem.come),
                            xfer(T.xs[:, cols(P)], 8 * chip + 2 + k, T.gw[:], 0xFF00, sem.fed)], local_sem=sem.sent)
        g.dma_start(T.land[:, blk(r)], T.x[:, blk(r)]).then_inc(sem.own, 16)
        g.wait_ge(sem.fed, 8)
        g.remote_dma_fused(deal(T.gw, 0, D, r - 2, 0) + on_chip, local_sem=sem.sent)

    g.wait_ge(sem.arrived, 32)
    g.wait_ge(sem.own, 16)
    g.dma_start(T.y[:], T.land[:]).then_inc(sem.stored, 16)
    g.wait_ge(sem.stored, 16)
    g.wait_ge(sem.sent, 32)
